import numpy as np
import ml_dtypes


def mxq(x, axis, fmt="e4m3"):
    dtype, down = {"e4m3": (ml_dtypes.float8_e4m3fn, 7), "e5m2": (ml_dtypes.float8_e5m2, 14)}[fmt]
    v = np.moveaxis(np.asarray(x, np.float32).astype(ml_dtypes.bfloat16).astype(np.float64), axis, -1)
    blocks = v.reshape(v.shape[:-1] + (-1, 32))
    amax = np.abs(blocks).max(-1, keepdims=True)
    byte = np.maximum(np.where(amax > 0, np.frexp(amax)[1] - 1 + 127, 0) - down, 1)
    scale = np.exp2(byte - 127.0)
    codes = (blocks / scale).astype(np.float32).astype(dtype).astype(np.float64)
    return np.moveaxis((codes * scale).reshape(v.shape), -1, axis)


WIDE = False


def mx_kscale(k):
    if not WIDE:
        return np.ones(k)
    levels = np.array([10, -10, 5, -5, 0])
    if k % 512:
        return np.exp2(np.random.permutation(np.resize(levels, k // 32))).repeat(32)
    a = np.empty((k // 512, 16))
    for p in range(k // 512):
        a[p, :8] = np.random.permutation(np.resize(levels, 8))
        for g in range(8):
            far = levels[np.abs(levels - a[p, g]) >= 10]
            a[p, g + 8] = far[np.random.randint(len(far))]
    return np.exp2(a.ravel()).repeat(32)


def f64(x):
    return np.asarray(x).astype(np.float64)


def striped(idx):
    return np.tile(idx.reshape(-1, 16).T, (8, 1)).astype(np.uint16)


def unstriped(offs):
    return offs[:16].T.reshape(-1).astype(np.int64)


K, T, N = 512, 512, 512


def setup_inputs():
    n = np.random.standard_normal
    s = mx_kscale(K)[:, None]
    idx = np.random.permutation(K)
    x = n((T, K))
    x[:, idx] *= s[:, 0]
    return {
        "x": x.astype(np.float32),
        "w": (n((K, N)) / np.sqrt(K) / s).astype(np.float32),
        "offs": striped(idx),
    }


def reference(x, w, offs):
    idx = unstriped(offs)
    xq = mxq(f64(x)[:, idx], 1, "e4m3").T
    return mxq(f64(w), 0, "e4m3").T @ xq

@@ -1,0 +1,173 @@
+from contextlib import ExitStack
+
+import concourse.mybir as mybir
+from concourse.masks import make_identity
+
+F32 = mybir.dt.float32
+BF16 = mybir.dt.bfloat16
+U32 = mybir.dt.uint32
+U16 = mybir.dt.uint16
+U8 = mybir.dt.uint8
+FP8X4 = mybir.dt.float8_e4m3fn_x4
+COPY = mybir.ActivationFunctionType.Copy
+MULT = mybir.AluOpType.mult
+ADD = mybir.AluOpType.add
+
+P = 128
+K = 512
+T = 512
+M = 512
+HALF = 256
+WINDOW = 704
+FLOPS = 2 * K * T * M
+
+
+def tile_picked_actorder_lin_none_perm_l_kernel(tc, x, w, offs, out):
+    nc = tc.nc
+    with ExitStack() as ctx:
+        held = ctx.enter_context(tc.tile_pool(name="held", bufs=1))
+        psum = ctx.enter_context(tc.psum_pool(name="psum", bufs=1))
+
+        offsets = held.tile([P, K // 16], U16, name="offsets")
+        nc.sync.dma_start(offsets[:], offs)
+
+        xs = []
+        for b in range(4):
+            xb = held.tile([P, WINDOW], F32, name="x%d" % b)
+            nc.sync.dma_start(out=xb[:, 0:K], in_=x[b * P : (b + 1) * P, :])
+            xs.append(xb)
+        w_raw = []
+        for c in range(2):
+            wc = held.tile([P, 4, HALF], F32, name="w_raw%d" % c)
+            nc.sync.dma_start(
+                out=wc[:], in_=w[:, c * HALF : (c + 1) * HALF].rearrange("(p j) m -> p j m", j=4)
+            )
+            w_raw.append(wc)
+
+        ident = held.tile([P, P], F32, name="ident")
+        make_identity(nc, ident[:])
+
+        grouped = [held.tile([P, P, 4], BF16, name="grouped%d" % b, align_bytes=64) for b in range(4)]
+        gathered = [held.tile([P, 2, P, 2], BF16, name="gathered%d" % b, align_bytes=64) for b in range(4)]
+        x_codes = held.tile([P, T], U32, name="x_codes", align_bytes=64)
+        x_scales = held.tile([P, T], U8, name="x_scales", align_bytes=64)
+        w_grouped = {}
+        w_codes = held.tile([P, M], U32, name="w_codes", align_bytes=64)
+        w_scales = held.tile([P, M], U8, name="w_scales", align_bytes=64)
+
+        x_bf = {}
+
+        def cast(b):
+            xc = held.tile([P, WINDOW], BF16, name="xbf%d" % b, align_bytes=64)
+            nc.gpsimd.tensor_scalar(xc[:, 0:K], xs[b][:, 0:K], 1.0, 0.0, MULT, ADD)
+            x_bf[b] = xc
+
+        def gather(b):
+            dst = gathered[b][:].rearrange("p u q e -> p q u e")
+            if b in x_bf:
+                nc.scalar.activation(dst, x_bf[b][:].indirect(offsets[:]), COPY)
+            else:
+                nc.vector.tensor_copy(dst, xs[b][:].indirect(offsets[:]))
+
+        xt = {}
+
+        def turn(b):
+            xt[b] = psum.tile([P, 2, P], F32, name="xt%d" % b)
+            for u in range(2):
+                nc.tensor.transpose(
+                    xt[b][:, u, :], gathered[b][:, u, :, :].rearrange("p q e -> p (q e)").bitcast(F32), ident[:]
+                )
+
+        def leave(b, engine):
+            dst = grouped[b][:].rearrange("p r t -> p (r t)").bitcast(F32)
+            src = xt[b][:].rearrange("p u r -> p r u")
+            if engine == "v":
+                nc.vector.tensor_copy(dst, src)
+            else:
+                nc.scalar.copy(dst, src)
+
+        def quant_x(b):
+            cols = slice(b * P, (b + 1) * P)
+            nc.vector.quantize_mx(
+                out=x_codes[:, cols].bitcast(FP8X4),
+                scales=x_scales[:, cols],
+                in_=grouped[b][:].rearrange("p r t -> p (r t)"),
+            )
+
+        def group_w(c, engine, slot):
+            w_grouped[c] = held.tile([P, P, 4], BF16, name=slot, align_bytes=64)
+            src = w_raw[c // 2][:, :, (c % 2) * P : (c % 2 + 1) * P].rearrange("p j m -> p m j")
+            if engine == "v":
+                nc.vector.tensor_copy(w_grouped[c][:], src)
+            elif engine == "g":
+                nc.gpsimd.tensor_scalar(w_grouped[c][:], src, 1.0, 0.0, MULT, ADD)
+            else:
+                nc.scalar.copy(w_grouped[c][:], src)
+
+        def quant_w(c):
+            cols = slice(c * P, (c + 1) * P)
+            nc.vector.quantize_mx(
+                out=w_codes[:, cols].bitcast(FP8X4),
+                scales=w_scales[:, cols],
+                in_=w_grouped[c][:].rearrange("p m j -> p (m j)"),
+            )
+
+        result = held.tile([P, 4, T], F32, name="result")
+
+        def product(c, first, width, bank, engine):
+            acc = psum.tile([P, width], F32, name=bank)
+            cols = slice(c * P, (c + 1) * P)
+            toks = slice(first, first + width)
+            nc.tensor.matmul_mx(
+                out=acc[:],
+                lhsT=w_codes[:, cols].bitcast(FP8X4),
+                lhsT_scale=w_scales[:, cols],
+                rhs=x_codes[:, toks].bitcast(FP8X4),
+                rhs_scale=x_scales[:, toks],
+                start=True,
+                stop=True,
+            )
+            if engine == "v":
+                nc.vector.tensor_copy(result[:, c, toks], acc[:])
+            else:
+                nc.scalar.copy(result[:, c, toks], acc[:])
+
+        def store(c):
+            nc.sync.dma_start(out=out[c * P : (c + 1) * P, :], in_=result[:, c, :])
+
+        gather(0)
+        cast(1)
+        cast(3)
+        gather(1)
+        turn(0)
+        gather(2)
+        group_w(0, "g", "wg0")
+        group_w(1, "g", "wg1")
+        turn(1)
+        gather(3)
+        turn(2)
+        leave(0, "v")
+        leave(1, "v")
+        quant_x(0)
+        leave(2, "v")
+        quant_x(1)
+        turn(3)
+        quant_x(2)
+        quant_w(0)
+        leave(3, "s")
+        quant_x(3)
+        group_w(2, "s", "gathered1")
+        product(0, 0, T, "acc0", "v")
+        quant_w(1)
+        group_w(3, "v", "gathered2")
+        product(1, 0, T, "acc1", "s")
+        quant_w(2)
+        store(0)
+        quant_w(3)
+        store(1)
+        product(2, 0, HALF, "acc2", "s")
+        product(2, HALF, HALF, "acc3", "v")
+        product(3, 0, HALF, "xt0", "s")
+        product(3, HALF, HALF, "xt1", "v")
+        store(2)
+        store(3)

@@ -31,45 +31,61 @@ def tile_picked_actorder_lin_none_perm_l_kernel(tc, x, w, offs, out):
         offsets = held.tile([P, K // 16], U16, name="offsets")
         nc.sync.dma_start(offsets[:], offs)
 
-        xs = []
-        for b in range(4):
-            xb = held.tile([P, WINDOW], F32, name="x%d" % b)
-            nc.sync.dma_start(out=xb[:, 0:K], in_=x[b * P : (b + 1) * P, :])
-            xs.append(xb)
-        w_raw = []
-        for c in range(2):
-            wc = held.tile([P, 4, HALF], F32, name="w_raw%d" % c)
+        xs = [held.tile([P, WINDOW], F32, name="x%d" % b) for b in range(4)]
+        w_raw = [held.tile([P, 4, HALF], F32, name="w_raw%d" % c) for c in range(2)]
+
+        def load_x(b):
+            nc.sync.dma_start(out=xs[b][:, 0:K], in_=x[b * P : (b + 1) * P, :])
+
+        def load_w(c):
             nc.sync.dma_start(
-                out=wc[:], in_=w[:, c * HALF : (c + 1) * HALF].rearrange("(p j) m -> p j m", j=4)
+                out=w_raw[c][:], in_=w[:, c * HALF : (c + 1) * HALF].rearrange("(p j) m -> p j m", j=4)
             )
-            w_raw.append(wc)
+
+        load_x(0)
+        load_x(1)
+        load_x(2)
+        load_x(3)
+        load_w(0)
+        load_w(1)
+
+        warm = held.tile([P, 2], F32, name="warm")
+        nc.vector.memset(warm[:, 0:1], 0.0)
+        nc.scalar.activation(warm[:, 1:2], warm[:, 0:1], COPY)
 
         ident = held.tile([P, P], F32, name="ident")
         make_identity(nc, ident[:])
 
-        grouped = [held.tile([P, P, 4], BF16, name="grouped%d" % b, align_bytes=64) for b in range(4)]
-        gathered = [held.tile([P, 2, P, 2], BF16, name="gathered%d" % b, align_bytes=64) for b in range(4)]
+        grouped = [held.tile([P, HALF, 4], BF16, name="grouped%d" % h, align_bytes=64) for h in range(2)]
+        gathered = {}
         x_codes = held.tile([P, T], U32, name="x_codes", align_bytes=64)
         x_scales = held.tile([P, T], U8, name="x_scales", align_bytes=64)
         w_grouped = {}
         w_codes = held.tile([P, M], U32, name="w_codes", align_bytes=64)
         w_scales = held.tile([P, M], U8, name="w_scales", align_bytes=64)
-
+        result = held.tile([P, 4, T], F32, name="result")
         x_bf = {}
+        xt = {}
 
-        def cast(b):
+        def cast(b, engine):
             xc = held.tile([P, WINDOW], BF16, name="xbf%d" % b, align_bytes=64)
-            nc.gpsimd.tensor_scalar(xc[:, 0:K], xs[b][:, 0:K], 1.0, 0.0, MULT, ADD)
+            if engine == "g":
+                nc.gpsimd.tensor_scalar(xc[:, 0:K], xs[b][:, 0:K], 1.0, 0.0, MULT, ADD)
+            elif engine == "v":
+                nc.vector.tensor_copy(xc[:, 0:K], xs[b][:, 0:K])
+            else:
+                nc.scalar.copy(xc[:, 0:K], xs[b][:, 0:K])
             x_bf[b] = xc
 
-        def gather(b):
-            dst = gathered[b][:].rearrange("p u q e -> p q u e")
-            if b in x_bf:
-                nc.scalar.activation(dst, x_bf[b][:].indirect(offsets[:]), COPY)
+        def gather(b, engine, first=0, last=P):
+            if b not in gathered:
+                gathered[b] = held.tile([P, 2, P, 2], BF16, name="gathered%d" % b, align_bytes=64)
+            dst = gathered[b][:, :, first:last, :].rearrange("p u q e -> p q u e")
+            lst = offsets[:, first // 4 : last // 4]
+            if engine == "s":
+                nc.scalar.activation(dst, x_bf[b][:].indirect(lst), COPY)
             else:
-                nc.vector.tensor_copy(dst, xs[b][:].indirect(offsets[:]))
-
-        xt = {}
+                nc.vector.tensor_copy(dst, xs[b][:].indirect(lst))
 
         def turn(b):
             xt[b] = psum.tile([P, 2, P], F32, name="xt%d" % b)
@@ -79,95 +95,110 @@ def tile_picked_actorder_lin_none_perm_l_kernel(tc, x, w, offs, out):
                 )
 
         def leave(b, engine):
-            dst = grouped[b][:].rearrange("p r t -> p (r t)").bitcast(F32)
+            rows = slice((b % 2) * P, (b % 2 + 1) * P)
+            dst = grouped[b // 2][:, rows, :].rearrange("p r t -> p (r t)").bitcast(F32)
             src = xt[b][:].rearrange("p u r -> p r u")
             if engine == "v":
                 nc.vector.tensor_copy(dst, src)
             else:
                 nc.scalar.copy(dst, src)
 
-        def quant_x(b):
-            cols = slice(b * P, (b + 1) * P)
+        def quant_x(first, last):
+            g = grouped[first // 2]
+            rows = slice((first % 2) * P, (last - first + first % 2) * P)
+            cols = slice(first * P, last * P)
             nc.vector.quantize_mx(
                 out=x_codes[:, cols].bitcast(FP8X4),
                 scales=x_scales[:, cols],
-                in_=grouped[b][:].rearrange("p r t -> p (r t)"),
+                in_=g[:, rows, :].rearrange("p r t -> p (r t)"),
             )
 
-        def group_w(c, engine, slot):
-            w_grouped[c] = held.tile([P, P, 4], BF16, name=slot, align_bytes=64)
-            src = w_raw[c // 2][:, :, (c % 2) * P : (c % 2 + 1) * P].rearrange("p j m -> p m j")
-            if engine == "v":
-                nc.vector.tensor_copy(w_grouped[c][:], src)
-            elif engine == "g":
-                nc.gpsimd.tensor_scalar(w_grouped[c][:], src, 1.0, 0.0, MULT, ADD)
-            else:
-                nc.scalar.copy(w_grouped[c][:], src)
+        def group_w(c, engine, slot, n=1):
+            w_grouped[c] = held.tile([P, n * P, 4], BF16, name=slot, align_bytes=64)
+            for i in range(n):
+                at = (c + i) % 2 * P
+                src = w_raw[c // 2][:, :, at : at + P].rearrange("p j m -> p m j")
+                dst = w_grouped[c][:, i * P : (i + 1) * P, :]
+                if engine[i] == "v":
+                    nc.vector.tensor_copy(dst, src)
+                elif engine[i] == "g":
+                    nc.gpsimd.tensor_scalar(dst, src, 1.0, 0.0, MULT, ADD)
+                else:
+                    nc.scalar.copy(dst, src)
 
-        def quant_w(c):
-            cols = slice(c * P, (c + 1) * P)
+        def quant_w(c, n=1):
+            cols = slice(c * P, (c + n) * P)
             nc.vector.quantize_mx(
                 out=w_codes[:, cols].bitcast(FP8X4),
                 scales=w_scales[:, cols],
                 in_=w_grouped[c][:].rearrange("p m j -> p (m j)"),
             )
 
-        result = held.tile([P, 4, T], F32, name="result")
-
-        def product(c, first, width, bank, engine):
-            acc = psum.tile([P, width], F32, name=bank)
-            cols = slice(c * P, (c + 1) * P)
+        def product(c, n, first, width, bank, engine):
+            acc = psum.tile([P, n, width], F32, name=bank)
             toks = slice(first, first + width)
-            nc.tensor.matmul_mx(
-                out=acc[:],
-                lhsT=w_codes[:, cols].bitcast(FP8X4),
-                lhsT_scale=w_scales[:, cols],
-                rhs=x_codes[:, toks].bitcast(FP8X4),
-                rhs_scale=x_scales[:, toks],
-                start=True,
-                stop=True,
-            )
+            for i in range(n):
+                cols = slice((c + i) * P, (c + i + 1) * P)
+                nc.tensor.matmul_mx(
+                    out=acc[:, i, :],
+                    lhsT=w_codes[:, cols].bitcast(FP8X4),
+                    lhsT_scale=w_scales[:, cols],
+                    rhs=x_codes[:, toks].bitcast(FP8X4),
+                    rhs_scale=x_scales[:, toks],
+                    start=True,
+                    stop=True,
+                )
+            return (acc, c, n, toks, engine)
+
+        def out_copy(job):
+            acc, c, n, toks, engine = job
             if engine == "v":
-                nc.vector.tensor_copy(result[:, c, toks], acc[:])
+                nc.vector.tensor_copy(result[:, c : c + n, toks], acc[:])
             else:
-                nc.scalar.copy(result[:, c, toks], acc[:])
+                nc.scalar.copy(result[:, c : c + n, toks], acc[:])
 
-        def store(c):
-            nc.sync.dma_start(out=out[c * P : (c + 1) * P, :], in_=result[:, c, :])
+        def store(c, n=1, first=0, last=T):
+            nc.sync.dma_start(
+                out=out[c * P : (c + n) * P, first:last].rearrange("(c p) t -> p c t", p=P),
+                in_=result[:, c : c + n, first:last],
+            )
 
-        gather(0)
-        cast(1)
-        cast(3)
-        gather(1)
+        gather(0, "v")
+        cast(1, "s")
+        gather(1, "s")
+        cast(3, "g")
         turn(0)
-        gather(2)
-        group_w(0, "g", "wg0")
-        group_w(1, "g", "wg1")
+        gather(2, "v")
         turn(1)
-        gather(3)
+        gather(3, "s", 0, 64)
+        gather(3, "v", 64, P)
+        group_w(0, "gg", "wg01", 2)
+        leave(0, "s")
+        leave(1, "s")
         turn(2)
-        leave(0, "v")
-        leave(1, "v")
-        quant_x(0)
         leave(2, "v")
-        quant_x(1)
         turn(3)
-        quant_x(2)
-        quant_w(0)
         leave(3, "s")
-        quant_x(3)
-        group_w(2, "s", "gathered1")
-        product(0, 0, T, "acc0", "v")
-        quant_w(1)
-        group_w(3, "v", "gathered2")
-        product(1, 0, T, "acc1", "s")
+        quant_x(0, 2)
+        quant_w(0, 2)
+        a = product(0, 2, 0, HALF, "accA", "v")
+        quant_x(2, 4)
+        group_w(2, "g", "wg2")
+        group_w(3, "s", "gathered3")
+        b = product(0, 2, HALF, HALF, "accB", "s")
         quant_w(2)
-        store(0)
+        out_copy(a)
+        store(0, 2, 0, HALF)
+        out_copy(b)
+        store(0, 2, HALF, T)
         quant_w(3)
-        store(1)
-        product(2, 0, HALF, "acc2", "s")
-        product(2, HALF, HALF, "acc3", "v")
-        product(3, 0, HALF, "xt0", "s")
-        product(3, HALF, HALF, "xt1", "v")
+        c = product(2, 1, 0, HALF, "accC", "s")
+        d = product(2, 1, HALF, HALF, "accD", "v")
+        e = product(3, 1, 0, HALF, "xt0", "s")
+        f = product(3, 1, HALF, HALF, "xt1", "v")
+        out_copy(c)
+        out_copy(d)
         store(2)
+        out_copy(e)
+        out_copy(f)
         store(3)

@@ -56,6 +56,12 @@ def tile_picked_actorder_lin_none_perm_l_kernel(tc, x, w, offs, out):
         ident = held.tile([P, P], F32, name="ident")
         make_identity(nc, ident[:])
 
+        spare = psum.tile([P, P], F32, name="spare")
+
+        def keep_busy(n):
+            for i in range(n):
+                nc.tensor.transpose(spare[:], ident[:], ident[:])
+
         grouped = [held.tile([P, HALF, 4], BF16, name="grouped%d" % h, align_bytes=64) for h in range(2)]
         gathered = {}
         x_codes = held.tile([P, T], U32, name="x_codes", align_bytes=64)
@@ -172,33 +178,35 @@ def tile_picked_actorder_lin_none_perm_l_kernel(tc, x, w, offs, out):
         turn(1)
         gather(3, "s", 0, 64)
         gather(3, "v", 64, P)
-        group_w(0, "gg", "wg01", 2)
+        group_w(0, "g", "wg0")
+        group_w(1, "g", "wg1")
         leave(0, "s")
         leave(1, "s")
         turn(2)
         leave(2, "v")
         turn(3)
+        quant_w(0)
         leave(3, "s")
         quant_x(0, 2)
-        quant_w(0, 2)
-        a = product(0, 2, 0, HALF, "accA", "v")
+        quant_w(1)
+        a = product(0, 2, 0, HALF, "accA", "s")
         quant_x(2, 4)
         group_w(2, "g", "wg2")
         group_w(3, "s", "gathered3")
-        b = product(0, 2, HALF, HALF, "accB", "s")
+        b = product(0, 2, HALF, HALF, "accB", "v")
         quant_w(2)
+        quant_w(3)
         out_copy(a)
         store(0, 2, 0, HALF)
         out_copy(b)
         store(0, 2, HALF, T)
-        quant_w(3)
-        c = product(2, 1, 0, HALF, "accC", "s")
-        d = product(2, 1, HALF, HALF, "accD", "v")
+        c = product(2, 1, 0, T, "accC", "v")
         e = product(3, 1, 0, HALF, "xt0", "s")
         f = product(3, 1, HALF, HALF, "xt1", "v")
         out_copy(c)
-        out_copy(d)
         store(2)
         out_copy(e)
+        store(3, 1, 0, HALF)
         out_copy(f)
-        store(3)
+        store(3, 1, HALF, T)
+        keep_busy(16)

@@ -35,7 +35,7 @@ def tile_picked_actorder_lin_none_perm_l_kernel(tc, x, w, offs, out):
         w_raw = [held.tile([P, 4, HALF], F32, name="w_raw%d" % c) for c in range(2)]
 
         def load_x(b):
-            nc.sync.dma_start(out=xs[b][:, 0:K], in_=x[b * P : (b + 1) * P, :])
+            (nc.scalar if b == 0 else nc.sync).dma_start(out=xs[b][:, 0:K], in_=x[b * P : (b + 1) * P, :])
 
         def load_w(c):
             nc.sync.dma_start(
@@ -55,12 +55,6 @@ def tile_picked_actorder_lin_none_perm_l_kernel(tc, x, w, offs, out):
 
         ident = held.tile([P, P], F32, name="ident")
         make_identity(nc, ident[:])
-
-        spare = psum.tile([P, P], F32, name="spare")
-
-        def keep_busy(n):
-            for i in range(n):
-                nc.tensor.transpose(spare[:], ident[:], ident[:])
 
         grouped = [held.tile([P, HALF, 4], BF16, name="grouped%d" % h, align_bytes=64) for h in range(2)]
         gathered = {}
@@ -190,23 +184,24 @@ def tile_picked_actorder_lin_none_perm_l_kernel(tc, x, w, offs, out):
         quant_x(0, 2)
         quant_w(1)
         a = product(0, 2, 0, HALF, "accA", "s")
-        quant_x(2, 4)
-        group_w(2, "g", "wg2")
-        group_w(3, "s", "gathered3")
-        b = product(0, 2, HALF, HALF, "accB", "v")
-        quant_w(2)
-        quant_w(3)
         out_copy(a)
         store(0, 2, 0, HALF)
+        group_w(3, "v", "gathered2")
+        quant_x(2, 4)
+        group_w(2, "g", "wg2")
+        b = product(0, 2, HALF, HALF, "accB", "s")
+        quant_w(2)
+        quant_w(3)
         out_copy(b)
         store(0, 2, HALF, T)
-        c = product(2, 1, 0, T, "accC", "v")
-        e = product(3, 1, 0, HALF, "xt0", "s")
-        f = product(3, 1, HALF, HALF, "xt1", "v")
+        c = product(2, 1, 0, HALF, "accC", "v")
+        d = product(2, 1, HALF, HALF, "accD", "s")
+        e = product(3, 1, 0, HALF, "xt0", "v")
+        f = product(3, 1, HALF, HALF, "xt1", "s")
         out_copy(c)
+        out_copy(d)
         store(2)
         out_copy(e)
         store(3, 1, 0, HALF)
         out_copy(f)
         store(3, 1, HALF, T)
-        keep_busy(16)

from contextlib import ExitStack

import concourse.mybir as mybir
from concourse.masks import make_identity

F32 = mybir.dt.float32
BF16 = mybir.dt.bfloat16
U32 = mybir.dt.uint32
U16 = mybir.dt.uint16
U8 = mybir.dt.uint8
FP8X4 = mybir.dt.float8_e4m3fn_x4
COPY = mybir.ActivationFunctionType.Copy
MULT = mybir.AluOpType.mult
ADD = mybir.AluOpType.add

P = 128
K = 512
T = 512
M = 512
HALF = 256
WINDOW = 704
FLOPS = 2 * K * T * M


def tile_picked_actorder_lin_none_perm_l_kernel(tc, x, w, offs, out):
    nc = tc.nc
    with ExitStack() as ctx:
        held = ctx.enter_context(tc.tile_pool(name="held", bufs=1))
        psum = ctx.enter_context(tc.psum_pool(name="psum", bufs=1))

        offsets = held.tile([P, K // 16], U16, name="offsets")
        nc.sync.dma_start(offsets[:], offs)

        xs = [held.tile([P, WINDOW], F32, name="x%d" % b) for b in range(4)]
        w_raw = [held.tile([P, 4, HALF], F32, name="w_raw%d" % c) for c in range(2)]

        def load_x(b):
            (nc.scalar if b == 0 else nc.sync).dma_start(out=xs[b][:, 0:K], in_=x[b * P : (b + 1) * P, :])

        def load_w(c):
            nc.sync.dma_start(
                out=w_raw[c][:], in_=w[:, c * HALF : (c + 1) * HALF].rearrange("(p j) m -> p j m", j=4)
            )

        load_x(0)
        load_x(1)
        load_x(2)
        load_x(3)
        load_w(0)
        load_w(1)

        warm = held.tile([P, 2], F32, name="warm")
        nc.vector.memset(warm[:, 0:1], 0.0)
        nc.scalar.activation(warm[:, 1:2], warm[:, 0:1], COPY)

        ident = held.tile([P, P], F32, name="ident")
        make_identity(nc, ident[:])

        grouped = [held.tile([P, HALF, 4], BF16, name="grouped%d" % h, align_bytes=64) for h in range(2)]
        gathered = {}
        x_codes = held.tile([P, T], U32, name="x_codes", align_bytes=64)
        x_scales = held.tile([P, T], U8, name="x_scales", align_bytes=64)
        w_grouped = {}
        w_codes = held.tile([P, M], U32, name="w_codes", align_bytes=64)
        w_scales = held.tile([P, M], U8, name="w_scales", align_bytes=64)
        result = held.tile([P, 4, T], F32, name="result")
        x_bf = {}
        xt = {}

        def cast(b, engine):
            xc = held.tile([P, WINDOW], BF16, name="xbf%d" % b, align_bytes=64)
            if engine == "g":
                nc.gpsimd.tensor_scalar(xc[:, 0:K], xs[b][:, 0:K], 1.0, 0.0, MULT, ADD)
            elif engine == "v":
                nc.vector.tensor_copy(xc[:, 0:K], xs[b][:, 0:K])
            else:
                nc.scalar.copy(xc[:, 0:K], xs[b][:, 0:K])
            x_bf[b] = xc

        def gather(b, engine, first=0, last=P):
            if b not in gathered:
                gathered[b] = held.tile([P, 2, P, 2], BF16, name="gathered%d" % b, align_bytes=64)
            dst = gathered[b][:, :, first:last, :].rearrange("p u q e -> p q u e")
            lst = offsets[:, first // 4 : last // 4]
            if engine == "s":
                nc.scalar.activation(dst, x_bf[b][:].indirect(lst), COPY)
            else:
                nc.vector.tensor_copy(dst, xs[b][:].indirect(lst))

        def turn(b):
            xt[b] = psum.tile([P, 2, P], F32, name="xt%d" % b)
            for u in range(2):
                nc.tensor.transpose(
                    xt[b][:, u, :], gathered[b][:, u, :, :].rearrange("p q e -> p (q e)").bitcast(F32), ident[:]
                )

        def leave(b, engine):
            rows = slice((b % 2) * P, (b % 2 + 1) * P)
            dst = grouped[b // 2][:, rows, :].rearrange("p r t -> p (r t)").bitcast(F32)
            src = xt[b][:].rearrange("p u r -> p r u")
            if engine == "v":
                nc.vector.tensor_copy(dst, src)
            else:
                nc.scalar.copy(dst, src)

        def quant_x(first, last):
            g = grouped[first // 2]
            rows = slice((first % 2) * P, (last - first + first % 2) * P)
            cols = slice(first * P, last * P)
            nc.vector.quantize_mx(
                out=x_codes[:, cols].bitcast(FP8X4),
                scales=x_scales[:, cols],
                in_=g[:, rows, :].rearrange("p r t -> p (r t)"),
            )

        def group_w(c, engine, slot, n=1):
            w_grouped[c] = held.tile([P, n * P, 4], BF16, name=slot, align_bytes=64)
            for i in range(n):
                at = (c + i) % 2 * P
                src = w_raw[c // 2][:, :, at : at + P].rearrange("p j m -> p m j")
                dst = w_grouped[c][:, i * P : (i + 1) * P, :]
                if engine[i] == "v":
                    nc.vector.tensor_copy(dst, src)
                elif engine[i] == "g":
                    nc.gpsimd.tensor_scalar(dst, src, 1.0, 0.0, MULT, ADD)
                else:
                    nc.scalar.copy(dst, src)

        def quant_w(c, n=1):
            cols = slice(c * P, (c + n) * P)
            nc.vector.quantize_mx(
                out=w_codes[:, cols].bitcast(FP8X4),
                scales=w_scales[:, cols],
                in_=w_grouped[c][:].rearrange("p m j -> p (m j)"),
            )

        def product(c, n, first, width, bank, engine):
            acc = psum.tile([P, n, width], F32, name=bank)
            toks = slice(first, first + width)
            for i in range(n):
                cols = slice((c + i) * P, (c + i + 1) * P)
                nc.tensor.matmul_mx(
                    out=acc[:, i, :],
                    lhsT=w_codes[:, cols].bitcast(FP8X4),
                    lhsT_scale=w_scales[:, cols],
                    rhs=x_codes[:, toks].bitcast(FP8X4),
                    rhs_scale=x_scales[:, toks],
                    start=True,
                    stop=True,
                )
            return (acc, c, n, toks, engine)

        def out_copy(job):
            acc, c, n, toks, engine = job
            if engine == "v":
                nc.vector.tensor_copy(result[:, c : c + n, toks], acc[:])
            else:
                nc.scalar.copy(result[:, c : c + n, toks], acc[:])

        def store(c, n=1, first=0, last=T):
            nc.sync.dma_start(
                out=out[c * P : (c + n) * P, first:last].rearrange("(c p) t -> p c t", p=P),
                in_=result[:, c : c + n, first:last],
            )

        gather(0, "v")
        cast(1, "s")
        gather(1, "s")
        cast(3, "g")
        turn(0)
        gather(2, "v")
        turn(1)
        gather(3, "s", 0, 64)
        gather(3, "v", 64, P)
        group_w(0, "g", "wg0")
        group_w(1, "g", "wg1")
        leave(0, "s")
        leave(1, "s")
        turn(2)
        leave(2, "v")
        turn(3)
        quant_w(0)
        leave(3, "s")
        quant_x(0, 2)
        quant_w(1)
        a = product(0, 2, 0, HALF, "accA", "s")
        out_copy(a)
        store(0, 2, 0, HALF)
        group_w(3, "v", "gathered2")
        quant_x(2, 4)
        group_w(2, "g", "wg2")
        b = product(0, 2, HALF, HALF, "accB", "s")
        quant_w(2)
        quant_w(3)
        out_copy(b)
        store(0, 2, HALF, T)
        c = product(2, 1, 0, HALF, "accC", "v")
        d = product(2, 1, HALF, HALF, "accD", "s")
        e = product(3, 1, 0, HALF, "xt0", "v")
        f = product(3, 1, HALF, HALF, "xt1", "s")
        out_copy(c)
        out_copy(d)
        store(2)
        out_copy(e)
        store(3, 1, 0, HALF)
        out_copy(f)
        store(3, 1, HALF, T)
